import numpy as np
import ml_dtypes


def mxq(x, axis, fmt="e4m3"):
    dtype, down = {"e4m3": (ml_dtypes.float8_e4m3fn, 7), "e5m2": (ml_dtypes.float8_e5m2, 14)}[fmt]
    v = np.moveaxis(np.asarray(x, np.float32).astype(ml_dtypes.bfloat16).astype(np.float64), axis, -1)
    blocks = v.reshape(v.shape[:-1] + (-1, 32))
    amax = np.abs(blocks).max(-1, keepdims=True)
    byte = np.maximum(np.where(amax > 0, np.frexp(amax)[1] - 1 + 127, 0) - down, 1)
    scale = np.exp2(byte - 127.0)
    codes = (blocks / scale).astype(np.float32).astype(dtype).astype(np.float64)
    return np.moveaxis((codes * scale).reshape(v.shape), -1, axis)


WIDE = False


def mx_kscale(k):
    if not WIDE:
        return np.ones(k)
    levels = np.array([10, -10, 5, -5, 0])
    if k % 512:
        return np.exp2(np.random.permutation(np.resize(levels, k // 32))).repeat(32)
    a = np.empty((k // 512, 16))
    for p in range(k // 512):
        a[p, :8] = np.random.permutation(np.resize(levels, 8))
        for g in range(8):
            far = levels[np.abs(levels - a[p, g]) >= 10]
            a[p, g + 8] = far[np.random.randint(len(far))]
    return np.exp2(a.ravel()).repeat(32)


def f64(x):
    return np.asarray(x).astype(np.float64)


def striped(idx):
    return np.tile(idx.reshape(-1, 16).T, (8, 1)).astype(np.uint16)


def unstriped(offs):
    return offs[:16].T.reshape(-1).astype(np.int64)


E2M1 = np.array([0.0, 0.5, 1.0, 1.5, 2.0, 3.0, 4.0, 6.0, -0.0, -0.5, -1.0, -1.5, -2.0, -3.0, -4.0, -6.0])


def pack_weight(w, fmt):
    k, n = w.shape
    w = f64(np.asarray(w, np.float32).astype(ml_dtypes.bfloat16)).reshape(k // 32, 32, n)
    amax = np.abs(w).max(1)
    if fmt == "e4m3":
        byte = np.frexp(amax)[1] - 1 + 127 - 7
    else:
        mant, ex = np.frexp(amax / 6.0)
        byte = np.where(mant > 0.5, ex, ex - 1) + 127
    byte = np.clip(np.where(amax > 0, byte, 1), 1, 254)
    scaled = (w * np.exp2(127.0 - byte)[:, None, :]).reshape(k, n).astype(np.float32)
    by_word = np.ascontiguousarray(scaled.reshape(k // 512, 128, 4, n).transpose(0, 1, 3, 2))
    if fmt == "e4m3":
        words = by_word.astype(ml_dtypes.float8_e4m3fn).view(np.uint8)
    else:
        c = by_word.astype(ml_dtypes.float4_e2m1fn).view(np.uint8) & 0xF
        words = (c[..., 0::2] | (c[..., 1::2] << 4)).reshape(k // 512, 128, 2 * n)
    return np.ascontiguousarray(words), np.ascontiguousarray(byte.astype(np.uint8).reshape(k // 512, 16, n))


def unpack_weight(words, scales, fmt):
    g, _, n = scales.shape
    words = np.ascontiguousarray(words).reshape(g, 128, n, -1)
    if fmt == "e4m3":
        vals = words.view(ml_dtypes.float8_e4m3fn).astype(np.float64)
    else:
        nib = np.empty((g, 128, n, 4), np.uint8)
        nib[..., 0::2] = words & 0xF
        nib[..., 1::2] = words >> 4
        vals = E2M1[nib]
    vals = vals * np.repeat(np.exp2(scales.astype(np.float64) - 127.0), 8, axis=1)[..., None]
    return vals.transpose(0, 1, 3, 2).reshape(g * 512, n)


def gelu(v):
    return 0.5 * v * (1.0 + np.tanh(np.sqrt(2.0 / np.pi) * (v + 0.044715 * v**3)))


def bf(x):
    return np.asarray(x, np.float32).astype(ml_dtypes.bfloat16)


def planes(Y):
    n, m = Y.shape
    b = f64(bf(Y)).reshape(n // 32, 32, m)
    amax = np.abs(b).max(1)
    byte = np.clip(np.where(amax > 0, np.frexp(amax)[1] - 1 + 127 - 7, 1), 1, 254)
    codes = (b * np.exp2(127.0 - byte)[:, None, :]).reshape(n, m).astype(np.float32).astype(ml_dtypes.float8_e4m3fn).view(np.uint8)
    words = codes.reshape(n // 512, 128, 4, m).transpose(0, 1, 3, 2)
    return np.ascontiguousarray(words), np.ascontiguousarray(byte.astype(np.uint8).reshape(n // 512, 16, m))


T, S, P, K, H, N = 4096, 1024, 512, 1024, 1024, 512


def setup_inputs():
    n = np.random.standard_normal
    s = mx_kscale(K)[:, None]
    u = mx_kscale(H)[:, None]
    size = np.exp(0.8 * n(N))
    d = {}
    d["tab_words"], d["tab_scales"] = pack_weight(n((K, T)) * s, "e4m3")
    d["offs"] = striped(np.random.permutation(T)[:S])
    d["w1"] = (n((K, H)) / K**0.5 / s).astype(np.float32)
    d["fold"] = (0.8 * n(H)).astype(np.float32)
    d["gain"] = (np.exp(0.3 * n(H)) * u[:, 0]).astype(np.float32)
    d["w4_words"], d["w4_scales"] = pack_weight(n((H, N)) / H**0.5 / u * size, "e2m1")
    d["wskip"] = (n((K, N)) / K**0.5 / s * size).astype(np.float32)
    d["base"] = (0.8 * n(N) * size).astype(np.float32)
    d["pos1"] = striped(np.random.permutation(S)[:P])
    d["pos2"] = striped(np.random.permutation(S)[:P])
    return d


def reference(tab_words, tab_scales, offs, w1, fold, gain, w4_words, w4_scales, wskip, base, pos1, pos2):
    v = unpack_weight(tab_words, tab_scales, "e4m3")[:, unstriped(offs)]
    a = mxq(f64(w1), 0, "e4m3").T @ v
    h = (a + f64(fold)[:, None] * np.abs(a)) * f64(gain)[:, None]
    hq = mxq(h, 0, "e4m3")
    w4 = unpack_weight(w4_words, w4_scales, "e2m1")
    ws = mxq(f64(wskip), 0, "e4m3")
    g2 = w4.T @ hq + ws.T @ v
    y = np.minimum(g2[:, unstriped(pos1)], g2[:, unstriped(pos2)]) + f64(base)[:, None]
    words, scales = planes(y)
    return y, words, scales

@@ -1,0 +1,283 @@
+from contextlib import ExitStack
+
+import concourse.mybir as mybir
+
+T, S, PAIRS, K, H, N = 4096, 1024, 512, 1024, 1024, 512
+FLOPS = 2 * S * (K * H + H * N + K * N)
+
+F32 = mybir.dt.float32
+BF16 = mybir.dt.bfloat16
+I32 = mybir.dt.int32
+U32 = mybir.dt.uint32
+U16 = mybir.dt.uint16
+U8 = mybir.dt.uint8
+FP8X4 = mybir.dt.float8_e4m3fn_x4
+FP4X4 = mybir.dt.float4_e2m1fn_x4
+ALU = mybir.AluOpType
+ACT = mybir.ActivationFunctionType
+
+P = 128
+PACK = 4
+KP = P * PACK
+BANK = 512
+UNIT = 256
+HALF = PAIRS // 2
+
+
+def tile_list_broadloom_shade_pairs_kernel(
+    tc, tab_words, tab_scales, offs, w1, fold, gain, w4_words, w4_scales, wskip, base, pos1, pos2,
+    out_0, out_1, out_2,
+):
+    nc = tc.nc
+    with ExitStack() as ctx:
+        keep = ctx.enter_context(tc.tile_pool(name="keep", bufs=1))
+        ring = ctx.enter_context(tc.tile_pool(name="ring", bufs=3))
+        psum = ctx.enter_context(tc.psum_pool(name="psum", bufs=8))
+
+        def held(shape, dtype, name):
+            return keep.tile(shape, dtype, name=name, align_bytes=64)
+
+        def passing(shape, dtype, name):
+            return ring.tile(shape, dtype, name=name, align_bytes=64)
+
+        idx = keep.tile([P, S // 16], U16, name="idx")
+        p1 = keep.tile([P, PAIRS // 16], U16, name="p1")
+        p2 = keep.tile([P, PAIRS // 16], U16, name="p2")
+
+        tab_plane = held([P, T], U8, "tab_plane")
+        w4_plane_raw = held([P, 2 * N], U8, "w4_plane_raw")
+        nc.vector.memset(tab_plane[:].bitcast(I32), 0)
+        nc.vector.memset(w4_plane_raw[:].bitcast(I32), 0)
+        fold_sb = held([P, 2, PACK], F32, "fold_sb")
+        gain_sb = held([P, 2, PACK], F32, "gain_sb")
+        base_sb = held([P, PACK], F32, "base_sb")
+        w4_raw = held([P, 2, 2 * N], U8, "w4_raw")
+        nc.scalar.dma_start(out=fold_sb[:], in_=fold.rearrange("(b p t) -> p b t", b=2, t=PACK))
+        nc.scalar.dma_start(out=gain_sb[:], in_=gain.rearrange("(b p t) -> p b t", b=2, t=PACK))
+        nc.scalar.dma_start(out=w4_raw[:].bitcast(I32), in_=w4_words.bitcast(I32).rearrange("a p c -> p a c"))
+        for q in range(4):
+            nc.scalar.dma_start(
+                out=tab_plane[32 * q : 32 * q + 8, :].bitcast(I32),
+                in_=tab_scales[:, 4 * q : 4 * q + 4, :].bitcast(I32),
+            )
+        for q in range(4):
+            nc.scalar.dma_start(
+                out=w4_plane_raw[32 * q : 32 * q + 4, :].bitcast(I32).rearrange("r (a c) -> r a c", a=2),
+                in_=w4_scales[:, 4 * q : 4 * q + 4, :].bitcast(I32).rearrange("a r c -> r a c"),
+            )
+
+        tab = [held([P, T], I32, "tab%d" % a) for a in range(2)]
+
+        def load_tab(a):
+            nc.sync.dma_start(out=tab[a][:], in_=tab_words[a].rearrange("p t i -> p (t i)").bitcast(I32))
+
+        def load_weight(w, a, c0, width, name):
+            raw = held([P, PACK, width], F32, name)
+            rows = w[KP * a : KP * (a + 1), c0 : c0 + width]
+            nc.sync.dma_start(out=raw[:], in_=rows.rearrange("(p j) c -> p j c", j=PACK))
+            return raw
+
+        nc.sync.dma_start(idx[:], offs)
+        load_tab(0)
+        load_tab(1)
+        w1_first = [[load_weight(w1, a, 256 * h, 256, "w1_raw0%d%d" % (a, h)) for h in range(2)] for a in range(2)]
+        w1_raw = {(1, a): load_weight(w1, a, KP, KP, "w1_raw1%d" % a) for a in range(2)}
+        ws_raw = [load_weight(wskip, a, 0, N, "ws_raw%d" % a) for a in range(2)]
+        nc.sync.dma_start(p1[:], pos1)
+        nc.sync.dma_start(p2[:], pos2)
+        nc.sync.dma_start(out=base_sb[:], in_=base.rearrange("(p t) -> p t", t=PACK))
+
+        w4_codes = held([P, 2, 2 * N], U8, "w4_codes")
+        w4_plane = held([P, 2, N], U8, "w4_plane")
+        for a in range(2):
+            nc.vector.tensor_copy(
+                out=w4_codes[:, a, :].rearrange("p (t m e) -> p m t e", t=PACK, e=2),
+                in_=w4_raw[:, a, :].rearrange("p (m t e) -> p m t e", t=PACK, e=2),
+            )
+        nc.vector.tensor_copy(
+            out=w4_plane[:].rearrange("p a (t m) -> p a m t", t=PACK),
+            in_=w4_plane_raw[:].rearrange("p (a m t) -> p a m t", a=2, t=PACK),
+        )
+        slope = held([P, 2, PACK], F32, "slope")
+        nc.vector.tensor_tensor(slope[:], fold_sb[:], gain_sb[:], ALU.mult)
+
+        def round_and_deal(copy, rounded, raw, m0):
+            count = raw[:].shape[2] // PACK
+            dst = rounded[:].rearrange("p (t m j) -> p m j t", t=PACK, j=PACK)
+            copy(out=dst[:, m0 : m0 + count], in_=raw[:].rearrange("p j (m t) -> p m j t", t=PACK))
+
+        def quantise(rounded, codes, plane):
+            nc.vector.quantize_mx(out=codes.bitcast(FP8X4), scales=plane, in_=rounded)
+
+        def weight_tiles(name):
+            return held([P, KP], U32, name + "_codes"), held([P, KP], U8, name + "_plane")
+
+        def new_rounded():
+            return passing([P, PACK * KP], BF16, "w_rounded")
+
+        v_words = [[held([P, BANK], U32, "v_words%d%d" % (a, c)) for c in range(2)] for a in range(2)]
+        v_plane = held([P, S], U8, "v_plane")
+
+        def gather_words(a, c):
+            window = tab[a][:].bitcast(U32)
+            nc.vector.tensor_copy(v_words[a][c][:], window.indirect(idx[:, 32 * c : 32 * (c + 1)]))
+
+        def v_operand(a, col0, width):
+            c, off = divmod(col0, BANK)
+            return v_words[a][c][:, off : off + width].bitcast(FP8X4), v_plane[4 * a :, col0 : col0 + width]
+
+        w1q = {(b, a): weight_tiles("w1q%d%d" % (b, a)) for b in range(2) for a in range(2)}
+        wsq = [weight_tiles("wsq%d" % a) for a in range(2)]
+
+        nc.vector.tensor_copy(v_plane[:], tab_plane[:].indirect(idx[:]))
+        gather_words(0, 0)
+        gather_words(0, 1)
+        gather_words(1, 0)
+        gather_words(1, 1)
+        for a in range(2):
+            rounded = new_rounded()
+            round_and_deal(nc.scalar.copy, rounded, w1_first[a][0], 0)
+            round_and_deal(nc.vector.tensor_copy, rounded, w1_first[a][1], 64)
+            quantise(rounded[:], w1q[0, a][0][:], w1q[0, a][1][:])
+
+        h_codes = {(b, c): held([P, BANK], U32, "h_codes%d%d" % (b, c)) for b in range(2) for c in range(2)}
+        h_plane = {(b, c): held([P, BANK], U8, "h_plane%d%d" % (b, c)) for b in range(2) for c in range(2)}
+
+        def response(b, col0):
+            banks = [psum.tile([P, PACK, P], F32, name="bank") for h in range(2)]
+            for a in range(2):
+                codes, plane = w1q[b, a]
+                for h in range(2):
+                    rhs, rhs_scale = v_operand(a, col0 + P * h, P)
+                    for t in range(PACK):
+                        nc.tensor.matmul_mx(
+                            out=banks[h][:, t, :],
+                            lhsT=codes[:, P * t : P * (t + 1)].bitcast(FP8X4),
+                            lhsT_scale=plane[:, P * t : P * (t + 1)],
+                            rhs=rhs,
+                            rhs_scale=rhs_scale,
+                            start=(a == 0 and t == 0),
+                            stop=(a == 1 and t == PACK - 1),
+                        )
+            sign = passing([P, PACK, UNIT], BF16, "sign")
+            for h in range(2):
+                nc.scalar.activation(sign[:, :, P * h : P * (h + 1)], banks[h][:], ACT.Sign)
+            factor = passing([P, PACK, UNIT], F32, "factor")
+            for t in range(PACK):
+                nc.scalar.activation(
+                    factor[:, t, :], sign[:, t, :], ACT.Identity,
+                    bias=gain_sb[:, b, t : t + 1], scale=slope[:, b, t : t + 1],
+                )
+            h_rounded = passing([P, UNIT, PACK], BF16, "h_rounded")
+            for h in range(2):
+                cols = slice(P * h, P * (h + 1))
+                nc.vector.tensor_tensor(
+                    h_rounded[:, cols, :].rearrange("p (c i) t -> p c t i", i=4),
+                    banks[h][:].rearrange("p t (c i) -> p c t i", i=4),
+                    factor[:, :, cols].rearrange("p t (c i) -> p c t i", i=4),
+                    ALU.mult,
+                )
+            return h_rounded
+
+        def quantise_response(b, col0, h_rounded):
+            c, off = divmod(col0, BANK)
+            quantise(
+                h_rounded[:].rearrange("p n t -> p (n t)"),
+                h_codes[b, c][:, off : off + UNIT],
+                h_plane[b, c][:, off : off + UNIT],
+            )
+
+        later = [(w1_raw[1, 0], w1q[1, 0]), (w1_raw[1, 1], w1q[1, 1]), (ws_raw[0], wsq[0]), (ws_raw[1], wsq[1])]
+        units = [(b, col0) for b in range(2) for col0 in range(0, S, UNIT)]
+        rounds_at = {0: 0, 1: 1, 4: 2, 5: 3}
+        waiting = []
+        for u, (b, col0) in enumerate(units):
+            ready = waiting
+            waiting = []
+            if u in rounds_at:
+                raw, tiles = later[rounds_at[u]]
+                rounded = new_rounded()
+                round_and_deal(nc.vector.tensor_copy, rounded, raw, 0)
+                waiting.append((rounded[:], tiles[0][:], tiles[1][:]))
+            h_rounded = response(b, col0)
+            for args in ready:
+                quantise(*args)
+            quantise_response(b, col0, h_rounded)
+
+        y = [held([P, PACK, HALF], F32, "y%d" % h) for h in range(2)]
+        y_codes = held([P, PAIRS], U32, "y_codes")
+        y_plane = held([P, PAIRS], U8, "y_plane")
+        out_rows = out_0.rearrange("(p t) m -> p t m", t=PACK)
+        out_words = out_1[0].rearrange("p m t -> p (m t)").bitcast(I32)
+
+        def features(t):
+            g2 = held([P, S], F32, "g2_%d" % t)
+            for c in range(2):
+                bank = psum.tile([P, BANK], F32, name="bank")
+                for a in range(2):
+                    rhs, rhs_scale = v_operand(a, BANK * c, BANK)
+                    nc.tensor.matmul_mx(
+                        out=bank[:],
+                        lhsT=wsq[a][0][:, P * t : P * (t + 1)].bitcast(FP8X4),
+                        lhsT_scale=wsq[a][1][:, P * t : P * (t + 1)],
+                        rhs=rhs,
+                        rhs_scale=rhs_scale,
+                        start=(a == 0),
+                        stop=False,
+                    )
+                for b in range(2):
+                    nc.tensor.matmul_mx(
+                        out=bank[:],
+                        lhsT=w4_codes[:, b, 2 * P * t : 2 * P * (t + 1)].bitcast(FP4X4),
+                        lhsT_scale=w4_plane[:, b, P * t : P * (t + 1)],
+                        rhs=h_codes[b, c][:].bitcast(FP8X4),
+                        rhs_scale=h_plane[b, c][:],
+                        start=False,
+                        stop=(b == 1),
+                    )
+                nc.scalar.copy(g2[:, BANK * c : BANK * (c + 1)], bank[:])
+            return g2
+
+        def pick(t, g2, m0, count):
+            first = passing([P, count], F32, "first")
+            second = passing([P, count], F32, "second")
+            raised = passing([P, count], F32, "raised")
+            cols = slice(m0 // 16, (m0 + count) // 16)
+            nc.vector.tensor_copy(first[:], g2[:].indirect(p1[:, cols]))
+            nc.vector.tensor_copy(second[:], g2[:].indirect(p2[:, cols]))
+            nc.scalar.activation(raised[:], first[:], ACT.Identity, bias=base_sb[:, t : t + 1])
+            for lo in range(0, count, HALF):
+                h = (m0 + lo) // HALF
+                nc.vector.scalar_tensor_tensor(
+                    y[h][:, t, :], second[:, lo : lo + HALF], base_sb[:, t : t + 1], raised[:, lo : lo + HALF],
+                    ALU.add, ALU.min,
+                )
+                nc.sync.dma_start(out=out_rows[:, t, HALF * h : HALF * (h + 1)], in_=y[h][:, t, :])
+
+        def round_pairs(copy, rounded, h, m0, count):
+            copy(
+                out=rounded[:, m0 : m0 + count, :].rearrange("p (c i) t -> p c t i", i=4),
+                in_=y[h][:, :, m0 : m0 + count].rearrange("p t (c i) -> p c t i", i=4),
+            )
+
+        def store_planes(h, rounded):
+            cols = slice(HALF * h, HALF * (h + 1))
+            quantise(rounded[:].rearrange("p m t -> p (m t)"), y_codes[:, cols], y_plane[:, cols])
+            nc.sync.dma_start(out=out_words[:, cols], in_=y_codes[:, cols].bitcast(I32))
+
+        g2 = [features(t) for t in range(PACK)]
+        for t in range(PACK - 1):
+            pick(t, g2[t], 0, PAIRS)
+        y_rounded = [held([P, HALF, PACK], BF16, "y_rounded%d" % h) for h in range(2)]
+        pick(PACK - 1, g2[PACK - 1], 0, HALF)
+        round_pairs(nc.scalar.copy, y_rounded[0], 0, 0, HALF)
+        pick(PACK - 1, g2[PACK - 1], HALF, HALF)
+        store_planes(0, y_rounded[0])
+        round_pairs(nc.vector.tensor_copy, y_rounded[1], 1, 0, HALF)
+        store_planes(1, y_rounded[1])
+        for q in range(4):
+            queue = nc.scalar if q % 2 == 0 else nc.sync
+            queue.dma_start(
+                out=out_2[0, 4 * q : 4 * q + 4, :].bitcast(I32),
+                in_=y_plane[32 * q : 32 * q + 4, :].bitcast(I32),
+            )

@@ -52,19 +52,6 @@ def tile_list_broadloom_shade_pairs_kernel(
         gain_sb = held([P, 2, PACK], F32, "gain_sb")
         base_sb = held([P, PACK], F32, "base_sb")
         w4_raw = held([P, 2, 2 * N], U8, "w4_raw")
-        nc.scalar.dma_start(out=fold_sb[:], in_=fold.rearrange("(b p t) -> p b t", b=2, t=PACK))
-        nc.scalar.dma_start(out=gain_sb[:], in_=gain.rearrange("(b p t) -> p b t", b=2, t=PACK))
-        nc.scalar.dma_start(out=w4_raw[:].bitcast(I32), in_=w4_words.bitcast(I32).rearrange("a p c -> p a c"))
-        for q in range(4):
-            nc.scalar.dma_start(
-                out=tab_plane[32 * q : 32 * q + 8, :].bitcast(I32),
-                in_=tab_scales[:, 4 * q : 4 * q + 4, :].bitcast(I32),
-            )
-        for q in range(4):
-            nc.scalar.dma_start(
-                out=w4_plane_raw[32 * q : 32 * q + 4, :].bitcast(I32).rearrange("r (a c) -> r a c", a=2),
-                in_=w4_scales[:, 4 * q : 4 * q + 4, :].bitcast(I32).rearrange("a r c -> r a c"),
-            )
 
         tab = [held([P, T], I32, "tab%d" % a) for a in range(2)]
 
@@ -78,10 +65,25 @@ def tile_list_broadloom_shade_pairs_kernel(
             return raw
 
         nc.sync.dma_start(idx[:], offs)
+        nc.sync.dma_start(out=w4_raw[:].bitcast(I32), in_=w4_words.bitcast(I32).rearrange("a p c -> p a c"))
         load_tab(0)
+        for q in range(4):
+            nc.sync.dma_start(
+                out=tab_plane[32 * q : 32 * q + 8, :].bitcast(I32),
+                in_=tab_scales[:, 4 * q : 4 * q + 4, :].bitcast(I32),
+            )
         load_tab(1)
-        w1_first = [[load_weight(w1, a, 256 * h, 256, "w1_raw0%d%d" % (a, h)) for h in range(2)] for a in range(2)]
-        w1_raw = {(1, a): load_weight(w1, a, KP, KP, "w1_raw1%d" % a) for a in range(2)}
+        w1_first = [[load_weight(w1, 0, 256 * h, 256, "w1_raw00%d" % h) for h in range(2)]]
+        nc.sync.dma_start(out=fold_sb[:], in_=fold.rearrange("(b p t) -> p b t", b=2, t=PACK))
+        nc.sync.dma_start(out=gain_sb[:], in_=gain.rearrange("(b p t) -> p b t", b=2, t=PACK))
+        w1_first.append([load_weight(w1, 1, 256 * h, 256, "w1_raw01%d" % h) for h in range(2)])
+        w1_raw = {(1, 0): load_weight(w1, 0, KP, KP, "w1_raw10")}
+        for q in range(4):
+            nc.sync.dma_start(
+                out=w4_plane_raw[32 * q : 32 * q + 4, :].bitcast(I32).rearrange("r (a c) -> r a c", a=2),
+                in_=w4_scales[:, 4 * q : 4 * q + 4, :].bitcast(I32).rearrange("a r c -> r a c"),
+            )
+        w1_raw[1, 1] = load_weight(w1, 1, KP, KP, "w1_raw11")
         ws_raw = [load_weight(wskip, a, 0, N, "ws_raw%d" % a) for a in range(2)]
         nc.sync.dma_start(p1[:], pos1)
         nc.sync.dma_start(p2[:], pos2)
@@ -91,20 +93,20 @@ def tile_list_broadloom_shade_pairs_kernel(
         w4_plane = held([P, 2, N], U8, "w4_plane")
         for a in range(2):
             nc.vector.tensor_copy(
-                out=w4_codes[:, a, :].rearrange("p (t m e) -> p m t e", t=PACK, e=2),
-                in_=w4_raw[:, a, :].rearrange("p (m t e) -> p m t e", t=PACK, e=2),
+                out=w4_codes[:, a, :].rearrange("p (t m e) -> p t m e", t=PACK, e=2),
+                in_=w4_raw[:, a, :].rearrange("p (m t e) -> p t m e", t=PACK, e=2),
             )
         nc.vector.tensor_copy(
-            out=w4_plane[:].rearrange("p a (t m) -> p a m t", t=PACK),
-            in_=w4_plane_raw[:].rearrange("p (a m t) -> p a m t", a=2, t=PACK),
+            out=w4_plane[:].rearrange("p a (t m) -> p a t m", t=PACK),
+            in_=w4_plane_raw[:].rearrange("p (a m t) -> p a t m", a=2, t=PACK),
         )
         slope = held([P, 2, PACK], F32, "slope")
         nc.vector.tensor_tensor(slope[:], fold_sb[:], gain_sb[:], ALU.mult)
 
         def round_and_deal(copy, rounded, raw, m0):
             count = raw[:].shape[2] // PACK
-            dst = rounded[:].rearrange("p (t m j) -> p m j t", t=PACK, j=PACK)
-            copy(out=dst[:, m0 : m0 + count], in_=raw[:].rearrange("p j (m t) -> p m j t", t=PACK))
+            dst = rounded[:].rearrange("p (u e m j) -> p u m j e", u=2, e=2, j=PACK)
+            copy(out=dst[:, :, m0 : m0 + count], in_=raw[:].rearrange("p j (m u e) -> p u m j e", u=2, e=2))
 
         def quantise(rounded, codes, plane):
             nc.vector.quantize_mx(out=codes.bitcast(FP8X4), scales=plane, in_=rounded)
@@ -129,9 +131,9 @@ def tile_list_broadloom_shade_pairs_kernel(
         w1q = {(b, a): weight_tiles("w1q%d%d" % (b, a)) for b in range(2) for a in range(2)}
         wsq = [weight_tiles("wsq%d" % a) for a in range(2)]
 
-        nc.vector.tensor_copy(v_plane[:], tab_plane[:].indirect(idx[:]))
         gather_words(0, 0)
         gather_words(0, 1)
+        nc.vector.tensor_copy(v_plane[:], tab_plane[:].indirect(idx[:]))
         gather_words(1, 0)
         gather_words(1, 1)
         for a in range(2):
@@ -143,15 +145,19 @@ def tile_list_broadloom_shade_pairs_kernel(
         h_codes = {(b, c): held([P, BANK], U32, "h_codes%d%d" % (b, c)) for b in range(2) for c in range(2)}
         h_plane = {(b, c): held([P, BANK], U8, "h_plane%d%d" % (b, c)) for b in range(2) for c in range(2)}
 
-        def response(b, col0):
-            banks = [psum.tile([P, PACK, P], F32, name="bank") for h in range(2)]
+        units = [(b, col0) for b in range(2) for col0 in range(0, S, UNIT)]
+        banks, signs, factors, h_rounded = {}, {}, {}, {}
+
+        def multiply(u):
+            b, col0 = units[u]
+            banks[u] = [psum.tile([P, PACK, P], F32, name="bank") for h in range(2)]
             for a in range(2):
                 codes, plane = w1q[b, a]
                 for h in range(2):
                     rhs, rhs_scale = v_operand(a, col0 + P * h, P)
                     for t in range(PACK):
                         nc.tensor.matmul_mx(
-                            out=banks[h][:, t, :],
+                            out=banks[u][h][:, t, :],
                             lhsT=codes[:, P * t : P * (t + 1)].bitcast(FP8X4),
                             lhsT_scale=plane[:, P * t : P * (t + 1)],
                             rhs=rhs,
@@ -159,50 +165,59 @@ def tile_list_broadloom_shade_pairs_kernel(
                             start=(a == 0 and t == 0),
                             stop=(a == 1 and t == PACK - 1),
                         )
-            sign = passing([P, PACK, UNIT], BF16, "sign")
-            for h in range(2):
-                nc.scalar.activation(sign[:, :, P * h : P * (h + 1)], banks[h][:], ACT.Sign)
-            factor = passing([P, PACK, UNIT], F32, "factor")
+            signs[u] = passing([P, PACK, UNIT], BF16, "sign")
+
+        def take_sign(u, h):
+            nc.scalar.activation(signs[u][:, :, P * h : P * (h + 1)], banks[u][h][:], ACT.Sign)
+
+        def make_factor(u):
+            b = units[u][0]
+            factors[u] = passing([P, PACK, UNIT], F32, "factor")
             for t in range(PACK):
                 nc.scalar.activation(
-                    factor[:, t, :], sign[:, t, :], ACT.Identity,
+                    factors[u][:, t, :], signs[u][:, t, :], ACT.Identity,
                     bias=gain_sb[:, b, t : t + 1], scale=slope[:, b, t : t + 1],
                 )
-            h_rounded = passing([P, UNIT, PACK], BF16, "h_rounded")
-            for h in range(2):
-                cols = slice(P * h, P * (h + 1))
-                nc.vector.tensor_tensor(
-                    h_rounded[:, cols, :].rearrange("p (c i) t -> p c t i", i=4),
-                    banks[h][:].rearrange("p t (c i) -> p c t i", i=4),
-                    factor[:, :, cols].rearrange("p t (c i) -> p c t i", i=4),
-                    ALU.mult,
-                )
-            return h_rounded
+            h_rounded[u] = passing([P, UNIT, PACK], BF16, "h_rounded")
 
-        def quantise_response(b, col0, h_rounded):
+        def bend(u, h):
+            cols = slice(P * h, P * (h + 1))
+            nc.vector.tensor_tensor(
+                h_rounded[u][:, cols, :].rearrange("p (c i) t -> p c t i", i=2),
+                banks[u][h][:].rearrange("p t (c i) -> p c t i", i=2),
+                factors[u][:, :, cols].rearrange("p t (c i) -> p c t i", i=2),
+                ALU.mult,
+            )
+
+        def quantise_response(u):
+            b, col0 = units[u]
             c, off = divmod(col0, BANK)
             quantise(
-                h_rounded[:].rearrange("p n t -> p (n t)"),
+                h_rounded[u][:].rearrange("p n t -> p (n t)"),
                 h_codes[b, c][:, off : off + UNIT],
                 h_plane[b, c][:, off : off + UNIT],
             )
 
-        later = [(w1_raw[1, 0], w1q[1, 0]), (w1_raw[1, 1], w1q[1, 1]), (ws_raw[0], wsq[0]), (ws_raw[1], wsq[1])]
-        units = [(b, col0) for b in range(2) for col0 in range(0, S, UNIT)]
-        rounds_at = {0: 0, 1: 1, 4: 2, 5: 3}
-        waiting = []
-        for u, (b, col0) in enumerate(units):
-            ready = waiting
-            waiting = []
-            if u in rounds_at:
-                raw, tiles = later[rounds_at[u]]
+        later = {0: (w1_raw[1, 0], w1q[1, 0]), 1: (w1_raw[1, 1], w1q[1, 1]), 4: (ws_raw[0], wsq[0]), 5: (ws_raw[1], wsq[1])}
+        multiply(0)
+        take_sign(0, 0)
+        for u in range(len(units)):
+            take_sign(u, 1)
+            if u + 1 < len(units):
+                multiply(u + 1)
+                take_sign(u + 1, 0)
+            make_factor(u)
+            if u in later:
+                raw, (codes, plane) = later[u]
                 rounded = new_rounded()
                 round_and_deal(nc.vector.tensor_copy, rounded, raw, 0)
-                waiting.append((rounded[:], tiles[0][:], tiles[1][:]))
-            h_rounded = response(b, col0)
-            for args in ready:
-                quantise(*args)
-            quantise_response(b, col0, h_rounded)
+            bend(u, 0)
+            if u > 0:
+                quantise_response(u - 1)
+            bend(u, 1)
+            if u in later:
+                quantise(rounded[:], codes[:], plane[:])
+        quantise_response(len(units) - 1)
 
         y = [held([P, PACK, HALF], F32, "y%d" % h) for h in range(2)]
         y_codes = held([P, PAIRS], U32, "y_codes")

@@ -44,16 +44,33 @@ def tile_list_broadloom_shade_pairs_kernel(
         p1 = keep.tile([P, PAIRS // 16], U16, name="p1")
         p2 = keep.tile([P, PAIRS // 16], U16, name="p2")
 
-        tab_plane = held([P, T], U8, "tab_plane")
-        w4_plane_raw = held([P, 2 * N], U8, "w4_plane_raw")
-        nc.vector.memset(tab_plane[:].bitcast(I32), 0)
-        nc.vector.memset(w4_plane_raw[:].bitcast(I32), 0)
+        tab_rows = held([P, T], U8, "tab_rows")
+        picked_rows = held([P, S], U8, "picked_rows")
+        v_plane = [held([P, S], U8, "v_plane%d" % a) for a in range(2)]
+        w4_rows = held([P, N], U8, "w4_rows")
+        w4_rows_dealt = held([P, N], U8, "w4_rows_dealt")
+        w4_plane = held([P, 2, N], U8, "w4_plane")
+        w4_raw = held([P, 2, 2 * N], U8, "w4_raw")
+        w4_codes = held([P, 2, 2 * N], U8, "w4_codes")
         fold_sb = held([P, 2, PACK], F32, "fold_sb")
         gain_sb = held([P, 2, PACK], F32, "gain_sb")
         base_sb = held([P, PACK], F32, "base_sb")
-        w4_raw = held([P, 2, 2 * N], U8, "w4_raw")
-
         tab = [held([P, T], I32, "tab%d" % a) for a in range(2)]
+        nc.gpsimd.memset(w4_rows[:].bitcast(I32), 0)
+        nc.gpsimd.memset(tab_rows[:, : T // 2].bitcast(I32), 0)
+        nc.vector.memset(tab_rows[:, T // 2 :].bitcast(I32), 0)
+        for plane in (v_plane[0], v_plane[1], w4_plane):
+            nc.vector.memset(plane[:].bitcast(I32), 0)
+
+        def load_rows(rows, scales):
+            nc.sync.dma_start(out=rows[0:P:4, :].bitcast(I32), in_=scales.rearrange("a q c -> (a q) c").bitcast(I32))
+
+        def place_rows(plane, rows, a):
+            for r in range(4):
+                nc.sync.dma_start(
+                    out=plane[r:P:32, :].bitcast(I32),
+                    in_=rows[64 * a + 4 * r : 64 * (a + 1) : 16, :].bitcast(I32),
+                )
 
         def load_tab(a):
             nc.sync.dma_start(out=tab[a][:], in_=tab_words[a].rearrange("p t i -> p (t i)").bitcast(I32))
@@ -64,49 +81,46 @@ def tile_list_broadloom_shade_pairs_kernel(
             nc.sync.dma_start(out=raw[:], in_=rows.rearrange("(p j) c -> p j c", j=PACK))
             return raw
 
+        def load_halves(b, a):
+            return [load_weight(w1, a, KP * b + 256 * h, 256, "w1_raw%d%d%d" % (b, a, h))[:] for h in range(2)]
+
         nc.sync.dma_start(idx[:], offs)
         nc.sync.dma_start(out=w4_raw[:].bitcast(I32), in_=w4_words.bitcast(I32).rearrange("a p c -> p a c"))
-        load_tab(0)
-        for q in range(4):
-            nc.sync.dma_start(
-                out=tab_plane[32 * q : 32 * q + 8, :].bitcast(I32),
-                in_=tab_scales[:, 4 * q : 4 * q + 4, :].bitcast(I32),
-            )
-        load_tab(1)
-        w1_first = [[load_weight(w1, 0, 256 * h, 256, "w1_raw00%d" % h) for h in range(2)]]
-        nc.sync.dma_start(out=fold_sb[:], in_=fold.rearrange("(b p t) -> p b t", b=2, t=PACK))
-        nc.sync.dma_start(out=gain_sb[:], in_=gain.rearrange("(b p t) -> p b t", b=2, t=PACK))
-        w1_first.append([load_weight(w1, 1, 256 * h, 256, "w1_raw01%d" % h) for h in range(2)])
-        w1_raw = {(1, 0): load_weight(w1, 0, KP, KP, "w1_raw10")}
-        for q in range(4):
-            nc.sync.dma_start(
-                out=w4_plane_raw[32 * q : 32 * q + 4, :].bitcast(I32).rearrange("r (a c) -> r a c", a=2),
-                in_=w4_scales[:, 4 * q : 4 * q + 4, :].bitcast(I32).rearrange("a r c -> r a c"),
-            )
-        w1_raw[1, 1] = load_weight(w1, 1, KP, KP, "w1_raw11")
-        ws_raw = [load_weight(wskip, a, 0, N, "ws_raw%d" % a) for a in range(2)]
         nc.sync.dma_start(p1[:], pos1)
-        nc.sync.dma_start(p2[:], pos2)
-        nc.sync.dma_start(out=base_sb[:], in_=base.rearrange("(p t) -> p t", t=PACK))
-
-        w4_codes = held([P, 2, 2 * N], U8, "w4_codes")
-        w4_plane = held([P, 2, N], U8, "w4_plane")
+        load_rows(w4_rows, w4_scales)
+        load_rows(tab_rows, tab_scales)
+        nc.vector.tensor_copy(picked_rows[:], tab_rows[:].indirect(idx[:]))
         for a in range(2):
             nc.vector.tensor_copy(
                 out=w4_codes[:, a, :].rearrange("p (t m e) -> p t m e", t=PACK, e=2),
                 in_=w4_raw[:, a, :].rearrange("p (m t e) -> p t m e", t=PACK, e=2),
             )
         nc.vector.tensor_copy(
-            out=w4_plane[:].rearrange("p a (t m) -> p a t m", t=PACK),
-            in_=w4_plane_raw[:].rearrange("p (a m t) -> p a t m", a=2, t=PACK),
+            out=w4_rows_dealt[:].rearrange("p (t m) -> p t m", t=PACK),
+            in_=w4_rows[:].rearrange("p (m t) -> p t m", t=PACK),
         )
+        load_tab(0)
+        load_tab(1)
+        place_rows(v_plane[0][:], picked_rows, 0)
+        whole = load_weight(w1, 0, 0, KP, "w1_raw00")
+        w1_first = [[whole[:, :, 0:256], whole[:, :, 256:512]], load_halves(0, 1)]
+        place_rows(v_plane[1][:], picked_rows, 1)
+        nc.sync.dma_start(out=fold_sb[:], in_=fold.rearrange("(b p t) -> p b t", b=2, t=PACK))
+        nc.sync.dma_start(out=gain_sb[:], in_=gain.rearrange("(b p t) -> p b t", b=2, t=PACK))
+        w1_raw = {(1, 0): load_halves(1, 0), (1, 1): [load_weight(w1, 1, KP, KP, "w1_raw11")[:]]}
+        ws_raw = [load_weight(wskip, a, 0, N, "ws_raw%d" % a)[:] for a in range(2)]
+        for a in range(2):
+            place_rows(w4_plane[:, a, :], w4_rows_dealt, a)
+        nc.sync.dma_start(p2[:], pos2)
+        nc.sync.dma_start(out=base_sb[:], in_=base.rearrange("(p t) -> p t", t=PACK))
+
         slope = held([P, 2, PACK], F32, "slope")
         nc.vector.tensor_tensor(slope[:], fold_sb[:], gain_sb[:], ALU.mult)
 
         def round_and_deal(copy, rounded, raw, m0):
-            count = raw[:].shape[2] // PACK
-            dst = rounded[:].rearrange("p (u e m j) -> p u m j e", u=2, e=2, j=PACK)
-            copy(out=dst[:, :, m0 : m0 + count], in_=raw[:].rearrange("p j (m u e) -> p u m j e", u=2, e=2))
+            count = raw.shape[2] // PACK
+            dst = rounded[:].rearrange("p (t m j) -> p m j t", t=PACK, j=PACK)
+            copy(out=dst[:, m0 : m0 + count], in_=raw.rearrange("p j (m t) -> p m j t", t=PACK))
 
         def quantise(rounded, codes, plane):
             nc.vector.quantize_mx(out=codes.bitcast(FP8X4), scales=plane, in_=rounded)
@@ -118,7 +132,6 @@ def tile_list_broadloom_shade_pairs_kernel(
             return passing([P, PACK * KP], BF16, "w_rounded")
 
         v_words = [[held([P, BANK], U32, "v_words%d%d" % (a, c)) for c in range(2)] for a in range(2)]
-        v_plane = held([P, S], U8, "v_plane")
 
         def gather_words(a, c):
             window = tab[a][:].bitcast(U32)
@@ -126,14 +139,13 @@ def tile_list_broadloom_shade_pairs_kernel(
 
         def v_operand(a, col0, width):
             c, off = divmod(col0, BANK)
-            return v_words[a][c][:, off : off + width].bitcast(FP8X4), v_plane[4 * a :, col0 : col0 + width]
+            return v_words[a][c][:, off : off + width].bitcast(FP8X4), v_plane[a][:, col0 : col0 + width]
 
         w1q = {(b, a): weight_tiles("w1q%d%d" % (b, a)) for b in range(2) for a in range(2)}
         wsq = [weight_tiles("wsq%d" % a) for a in range(2)]
 
         gather_words(0, 0)
         gather_words(0, 1)
-        nc.vector.tensor_copy(v_plane[:], tab_plane[:].indirect(idx[:]))
         gather_words(1, 0)
         gather_words(1, 1)
         for a in range(2):
@@ -183,9 +195,9 @@ def tile_list_broadloom_shade_pairs_kernel(
         def bend(u, h):
             cols = slice(P * h, P * (h + 1))
             nc.vector.tensor_tensor(
-                h_rounded[u][:, cols, :].rearrange("p (c i) t -> p c t i", i=2),
-                banks[u][h][:].rearrange("p t (c i) -> p c t i", i=2),
-                factors[u][:, :, cols].rearrange("p t (c i) -> p c t i", i=2),
+                h_rounded[u][:, cols, :].rearrange("p (c i) t -> p c t i", i=4),
+                banks[u][h][:].rearrange("p t (c i) -> p c t i", i=4),
+                factors[u][:, :, cols].rearrange("p t (c i) -> p c t i", i=4),
                 ALU.mult,
             )
 
@@ -198,7 +210,7 @@ def tile_list_broadloom_shade_pairs_kernel(
                 h_plane[b, c][:, off : off + UNIT],
             )
 
-        later = {0: (w1_raw[1, 0], w1q[1, 0]), 1: (w1_raw[1, 1], w1q[1, 1]), 4: (ws_raw[0], wsq[0]), 5: (ws_raw[1], wsq[1])}
+        later = {0: (w1_raw[1, 0], w1q[1, 0]), 1: (w1_raw[1, 1], w1q[1, 1]), 3: ([ws_raw[0]], wsq[0]), 4: ([ws_raw[1]], wsq[1])}
         multiply(0)
         take_sign(0, 0)
         for u in range(len(units)):
@@ -210,7 +222,8 @@ def tile_list_broadloom_shade_pairs_kernel(
             if u in later:
                 raw, (codes, plane) = later[u]
                 rounded = new_rounded()
-                round_and_deal(nc.vector.tensor_copy, rounded, raw, 0)
+                for h, piece in enumerate(raw):
+                    round_and_deal(nc.vector.tensor_copy, rounded, piece, 64 * h)
             bend(u, 0)
             if u > 0:
                 quantise_response(u - 1)

@@ -56,10 +56,7 @@ def tile_list_broadloom_shade_pairs_kernel(
         gain_sb = held([P, 2, PACK], F32, "gain_sb")
         base_sb = held([P, PACK], F32, "base_sb")
         tab = [held([P, T], I32, "tab%d" % a) for a in range(2)]
-        nc.gpsimd.memset(w4_rows[:].bitcast(I32), 0)
-        nc.gpsimd.memset(tab_rows[:, : T // 2].bitcast(I32), 0)
-        nc.vector.memset(tab_rows[:, T // 2 :].bitcast(I32), 0)
-        for plane in (v_plane[0], v_plane[1], w4_plane):
+        for plane in (tab_rows, w4_rows, v_plane[0], v_plane[1], w4_plane):
             nc.vector.memset(plane[:].bitcast(I32), 0)
 
         def load_rows(rows, scales):
@@ -86,9 +83,10 @@ def tile_list_broadloom_shade_pairs_kernel(
 
         nc.sync.dma_start(idx[:], offs)
         nc.sync.dma_start(out=w4_raw[:].bitcast(I32), in_=w4_words.bitcast(I32).rearrange("a p c -> p a c"))
-        nc.sync.dma_start(p1[:], pos1)
-        load_rows(w4_rows, w4_scales)
+        nc.sync.dma_start(out=fold_sb[:], in_=fold.rearrange("(b p t) -> p b t", b=2, t=PACK))
+        nc.sync.dma_start(out=gain_sb[:], in_=gain.rearrange("(b p t) -> p b t", b=2, t=PACK))
         load_rows(tab_rows, tab_scales)
+        load_rows(w4_rows, w4_scales)
         nc.vector.tensor_copy(picked_rows[:], tab_rows[:].indirect(idx[:]))
         for a in range(2):
             nc.vector.tensor_copy(
@@ -102,25 +100,24 @@ def tile_list_broadloom_shade_pairs_kernel(
         load_tab(0)
         load_tab(1)
         place_rows(v_plane[0][:], picked_rows, 0)
-        whole = load_weight(w1, 0, 0, KP, "w1_raw00")
-        w1_first = [[whole[:, :, 0:256], whole[:, :, 256:512]], load_halves(0, 1)]
+        w1_first = [[load_weight(w1, 0, 0, KP, "w1_raw00")[:]], load_halves(0, 1)]
         place_rows(v_plane[1][:], picked_rows, 1)
-        nc.sync.dma_start(out=fold_sb[:], in_=fold.rearrange("(b p t) -> p b t", b=2, t=PACK))
-        nc.sync.dma_start(out=gain_sb[:], in_=gain.rearrange("(b p t) -> p b t", b=2, t=PACK))
         w1_raw = {(1, 0): load_halves(1, 0), (1, 1): [load_weight(w1, 1, KP, KP, "w1_raw11")[:]]}
         ws_raw = [load_weight(wskip, a, 0, N, "ws_raw%d" % a)[:] for a in range(2)]
         for a in range(2):
             place_rows(w4_plane[:, a, :], w4_rows_dealt, a)
+        nc.sync.dma_start(p1[:], pos1)
         nc.sync.dma_start(p2[:], pos2)
         nc.sync.dma_start(out=base_sb[:], in_=base.rearrange("(p t) -> p t", t=PACK))
 
         slope = held([P, 2, PACK], F32, "slope")
         nc.vector.tensor_tensor(slope[:], fold_sb[:], gain_sb[:], ALU.mult)
 
-        def round_and_deal(copy, rounded, raw, m0):
+        def round_and_deal(copy, rounded, raw, m0, slices):
             count = raw.shape[2] // PACK
             dst = rounded[:].rearrange("p (t m j) -> p m j t", t=PACK, j=PACK)
-            copy(out=dst[:, m0 : m0 + count], in_=raw.rearrange("p j (m t) -> p m j t", t=PACK))
+            src = raw.rearrange("p j (m t) -> p m j t", t=PACK)
+            copy(out=dst[:, m0 : m0 + count, :, slices], in_=src[:, :, :, slices])
 
         def quantise(rounded, codes, plane):
             nc.vector.quantize_mx(out=codes.bitcast(FP8X4), scales=plane, in_=rounded)
@@ -150,15 +147,26 @@ def tile_list_broadloom_shade_pairs_kernel(
         gather_words(1, 1)
         for a in range(2):
             rounded = new_rounded()
-            round_and_deal(nc.scalar.copy, rounded, w1_first[a][0], 0)
-            round_and_deal(nc.vector.tensor_copy, rounded, w1_first[a][1], 64)
-            quantise(rounded[:], w1q[0, a][0][:], w1q[0, a][1][:])
+            for h, piece in enumerate(w1_first[a]):
+                if a == 0:
+                    round_and_deal(nc.vector.tensor_copy, rounded, piece, 0, slice(0, 4))
+                else:
+                    round_and_deal(nc.scalar.copy, rounded, piece, 64 * h, slice(0, 2))
+                    round_and_deal(nc.vector.tensor_copy, rounded, piece, 64 * h, slice(2, 4))
+            if a == 0:
+                quantise(rounded[:], w1q[0, a][0][:], w1q[0, a][1][:])
+            else:
+                for lo in (256, 0):
+                    quantise(rounded[:, 4 * lo : 4 * lo + 1024], w1q[0, a][0][:, lo : lo + 256], w1q[0, a][1][:, lo : lo + 256])
 
         h_codes = {(b, c): held([P, BANK], U32, "h_codes%d%d" % (b, c)) for b in range(2) for c in range(2)}
         h_plane = {(b, c): held([P, BANK], U8, "h_plane%d%d" % (b, c)) for b in range(2) for c in range(2)}
 
         units = [(b, col0) for b in range(2) for col0 in range(0, S, UNIT)]
         banks, signs, factors, h_rounded = {}, {}, {}, {}
+
+        def new_quarter():
+            return ring.tile([P, UNIT * PACK], BF16, name="to_quantise", align_bytes=64, bufs=2)
 
         def multiply(u):
             b, col0 = units[u]
@@ -186,11 +194,17 @@ def tile_list_broadloom_shade_pairs_kernel(
             b = units[u][0]
             factors[u] = passing([P, PACK, UNIT], F32, "factor")
             for t in range(PACK):
-                nc.scalar.activation(
-                    factors[u][:, t, :], signs[u][:, t, :], ACT.Identity,
-                    bias=gain_sb[:, b, t : t + 1], scale=slope[:, b, t : t + 1],
-                )
-            h_rounded[u] = passing([P, UNIT, PACK], BF16, "h_rounded")
+                if u in (0, len(units) - 1):
+                    nc.vector.tensor_scalar(
+                        factors[u][:, t, :], signs[u][:, t, :], slope[:, b, t : t + 1], gain_sb[:, b, t : t + 1],
+                        ALU.mult, ALU.add,
+                    )
+                else:
+                    nc.scalar.activation(
+                        factors[u][:, t, :], signs[u][:, t, :], ACT.Identity,
+                        bias=gain_sb[:, b, t : t + 1], scale=slope[:, b, t : t + 1],
+                    )
+            h_rounded[u] = new_quarter()[:].rearrange("p (n t) -> p n t", t=PACK)
 
         def bend(u, h):
             cols = slice(P * h, P * (h + 1))
@@ -205,12 +219,25 @@ def tile_list_broadloom_shade_pairs_kernel(
             b, col0 = units[u]
             c, off = divmod(col0, BANK)
             quantise(
-                h_rounded[u][:].rearrange("p n t -> p (n t)"),
+                h_rounded[u].rearrange("p n t -> p (n t)"),
                 h_codes[b, c][:, off : off + UNIT],
                 h_plane[b, c][:, off : off + UNIT],
             )
 
-        later = {0: (w1_raw[1, 0], w1q[1, 0]), 1: (w1_raw[1, 1], w1q[1, 1]), 3: ([ws_raw[0]], wsq[0]), 4: ([ws_raw[1]], wsq[1])}
+
+        def round_w1(a):
+            rounded = new_rounded()
+            for h, piece in enumerate(w1_raw[1, a]):
+                round_and_deal(nc.vector.tensor_copy, rounded, piece, 64 * h, slice(0, PACK))
+            return rounded[:], w1q[1, a][0][:], w1q[1, a][1][:]
+
+        def round_wskip(copy, rounded, a, pair):
+            dst = rounded[:].rearrange("p (t m j) -> p m j t", t=2, j=PACK)
+            src = ws_raw[a].rearrange("p j (m t) -> p m j t", t=PACK)
+            copy(out=dst, in_=src[:, :, :, 2 * pair : 2 * pair + 2])
+            cols = slice(2 * P * pair, 2 * P * (pair + 1))
+            return rounded[:], wsq[a][0][:, cols], wsq[a][1][:, cols]
+
         multiply(0)
         take_sign(0, 0)
         for u in range(len(units)):
@@ -219,20 +246,23 @@ def tile_list_broadloom_shade_pairs_kernel(
                 multiply(u + 1)
                 take_sign(u + 1, 0)
             make_factor(u)
-            if u in later:
-                raw, (codes, plane) = later[u]
-                rounded = new_rounded()
-                for h, piece in enumerate(raw):
-                    round_and_deal(nc.vector.tensor_copy, rounded, piece, 64 * h)
+            weight = None
+            if u in (0, 1):
+                weight = round_w1(u)
+            if u in (3, 4):
+                weight = round_wskip(nc.vector.tensor_copy, passing([P, UNIT * PACK], BF16, "ws_rounded"), u - 3, 0)
             bend(u, 0)
             if u > 0:
                 quantise_response(u - 1)
             bend(u, 1)
-            if u in later:
-                quantise(rounded[:], codes[:], plane[:])
+            if weight is not None:
+                quantise(*weight)
         quantise_response(len(units) - 1)
+        late = [round_wskip(nc.scalar.copy, new_quarter(), 0, 1), round_wskip(nc.vector.tensor_copy, new_quarter(), 1, 1)]
+        for weight in late:
+            quantise(*weight)
 
-        y = [held([P, PACK, HALF], F32, "y%d" % h) for h in range(2)]
+        y = held([P, 2, PACK, HALF], F32, "y")
         y_codes = held([P, PAIRS], U32, "y_codes")
         y_plane = held([P, PAIRS], U8, "y_plane")
         out_rows = out_0.rearrange("(p t) m -> p t m", t=PACK)
@@ -274,18 +304,21 @@ def tile_list_broadloom_shade_pairs_kernel(
             nc.vector.tensor_copy(first[:], g2[:].indirect(p1[:, cols]))
             nc.vector.tensor_copy(second[:], g2[:].indirect(p2[:, cols]))
             nc.scalar.activation(raised[:], first[:], ACT.Identity, bias=base_sb[:, t : t + 1])
-            for lo in range(0, count, HALF):
-                h = (m0 + lo) // HALF
-                nc.vector.scalar_tensor_tensor(
-                    y[h][:, t, :], second[:, lo : lo + HALF], base_sb[:, t : t + 1], raised[:, lo : lo + HALF],
-                    ALU.add, ALU.min,
-                )
-                nc.sync.dma_start(out=out_rows[:, t, HALF * h : HALF * (h + 1)], in_=y[h][:, t, :])
+            halves = y[:, m0 // HALF : (m0 + count) // HALF, t, :]
+            nc.vector.scalar_tensor_tensor(
+                halves,
+                second[:].rearrange("p (h m) -> p h m", m=HALF),
+                base_sb[:, t : t + 1],
+                raised[:].rearrange("p (h m) -> p h m", m=HALF),
+                ALU.add,
+                ALU.min,
+            )
+            nc.sync.dma_start(out=out_rows[:, t, m0 : m0 + count].rearrange("p (h m) -> p h m", m=HALF), in_=halves)
 
         def round_pairs(copy, rounded, h, m0, count):
             copy(
                 out=rounded[:, m0 : m0 + count, :].rearrange("p (c i) t -> p c t i", i=4),
-                in_=y[h][:, :, m0 : m0 + count].rearrange("p t (c i) -> p c t i", i=4),
+                in_=y[:, h, :, m0 : m0 + count].rearrange("p t (c i) -> p c t i", i=4),
             )
 
         def store_planes(h, rounded):

@@ -19,9 +19,18 @@ ACT = mybir.ActivationFunctionType
 P = 128
 PACK = 4
 KP = P * PACK
+PASSES = 2
 BANK = 512
-UNIT = 256
+LIST = 16
+QUADS = 4
+STEP = 2 * P
 HALF = PAIRS // 2
+PIECE = KP // 2
+RUN = 4
+LOW, HIGH, ALL = slice(0, 2), slice(2, PACK), slice(0, PACK)
+VECTOR_SHARE = 168
+W1_STEPS = (0, 1)
+WSKIP_STEPS = (3, 4)
 
 
 def tile_list_broadloom_shade_pairs_kernel(
@@ -40,24 +49,24 @@ def tile_list_broadloom_shade_pairs_kernel(
         def passing(shape, dtype, name):
             return ring.tile(shape, dtype, name=name, align_bytes=64)
 
-        idx = keep.tile([P, S // 16], U16, name="idx")
-        p1 = keep.tile([P, PAIRS // 16], U16, name="p1")
-        p2 = keep.tile([P, PAIRS // 16], U16, name="p2")
+        idx = keep.tile([P, S // LIST], U16, name="idx")
+        p1 = keep.tile([P, PAIRS // LIST], U16, name="p1")
+        p2 = keep.tile([P, PAIRS // LIST], U16, name="p2")
 
         tab_rows = held([P, T], U8, "tab_rows")
         picked_rows = held([P, S], U8, "picked_rows")
-        v_plane = [held([P, S], U8, "v_plane%d" % a) for a in range(2)]
+        v_plane = [held([P, S], U8, "v_plane%d" % a) for a in range(PASSES)]
         w4_rows = held([P, N], U8, "w4_rows")
         w4_rows_dealt = held([P, N], U8, "w4_rows_dealt")
-        w4_plane = held([P, 2, N], U8, "w4_plane")
-        w4_raw = held([P, 2, 2 * N], U8, "w4_raw")
-        w4_codes = held([P, 2, 2 * N], U8, "w4_codes")
-        fold_sb = held([P, 2, PACK], F32, "fold_sb")
-        gain_sb = held([P, 2, PACK], F32, "gain_sb")
+        w4_plane = held([P, PASSES, N], U8, "w4_plane")
+        w4_raw = held([P, PASSES, 2 * N], U8, "w4_raw")
+        w4_codes = held([P, PASSES, 2 * N], U8, "w4_codes")
+        fold_sb = held([P, PASSES, PACK], F32, "fold_sb")
+        gain_sb = held([P, PASSES, PACK], F32, "gain_sb")
         base_sb = held([P, PACK], F32, "base_sb")
-        tab = [held([P, T], I32, "tab%d" % a) for a in range(2)]
-        for plane in (tab_rows, w4_rows, v_plane[0], v_plane[1], w4_plane):
-            nc.vector.memset(plane[:].bitcast(I32), 0)
+        tab = [held([P, T], I32, "tab%d" % a) for a in range(PASSES)]
+        for partly_loaded in (tab_rows, w4_rows, v_plane[0], v_plane[1], w4_plane):
+            nc.vector.memset(partly_loaded[:].bitcast(I32), 0)
 
         def load_rows(rows, scales):
             nc.sync.dma_start(out=rows[0:P:4, :].bitcast(I32), in_=scales.rearrange("a q c -> (a q) c").bitcast(I32))
@@ -76,22 +85,25 @@ def tile_list_broadloom_shade_pairs_kernel(
             raw = held([P, PACK, width], F32, name)
             rows = w[KP * a : KP * (a + 1), c0 : c0 + width]
             nc.sync.dma_start(out=raw[:], in_=rows.rearrange("(p j) c -> p j c", j=PACK))
-            return raw
+            return raw[:]
 
-        def load_halves(b, a):
-            return [load_weight(w1, a, KP * b + 256 * h, 256, "w1_raw%d%d%d" % (b, a, h))[:] for h in range(2)]
+        def load_w1(b, a):
+            return [load_weight(w1, a, KP * b, KP, "w1_raw%d%d" % (b, a))]
+
+        def load_w1_pieces(b, a):
+            return [load_weight(w1, a, KP * b + PIECE * i, PIECE, "w1_raw%d%d%d" % (b, a, i)) for i in range(2)]
 
         nc.sync.dma_start(idx[:], offs)
         nc.sync.dma_start(out=w4_raw[:].bitcast(I32), in_=w4_words.bitcast(I32).rearrange("a p c -> p a c"))
-        nc.sync.dma_start(out=fold_sb[:], in_=fold.rearrange("(b p t) -> p b t", b=2, t=PACK))
-        nc.sync.dma_start(out=gain_sb[:], in_=gain.rearrange("(b p t) -> p b t", b=2, t=PACK))
+        nc.sync.dma_start(out=fold_sb[:], in_=fold.rearrange("(b p t) -> p b t", b=PASSES, t=PACK))
+        nc.sync.dma_start(out=gain_sb[:], in_=gain.rearrange("(b p t) -> p b t", b=PASSES, t=PACK))
         load_rows(tab_rows, tab_scales)
         load_rows(w4_rows, w4_scales)
         nc.vector.tensor_copy(picked_rows[:], tab_rows[:].indirect(idx[:]))
-        for a in range(2):
+        for b in range(PASSES):
             nc.vector.tensor_copy(
-                out=w4_codes[:, a, :].rearrange("p (t m e) -> p t m e", t=PACK, e=2),
-                in_=w4_raw[:, a, :].rearrange("p (m t e) -> p t m e", t=PACK, e=2),
+                out=w4_codes[:, b, :].rearrange("p (t m e) -> p t m e", t=PACK, e=2),
+                in_=w4_raw[:, b, :].rearrange("p (m t e) -> p t m e", t=PACK, e=2),
             )
         nc.vector.tensor_copy(
             out=w4_rows_dealt[:].rearrange("p (t m) -> p t m", t=PACK),
@@ -100,17 +112,18 @@ def tile_list_broadloom_shade_pairs_kernel(
         load_tab(0)
         load_tab(1)
         place_rows(v_plane[0][:], picked_rows, 0)
-        w1_first = [[load_weight(w1, 0, 0, KP, "w1_raw00")[:]], load_halves(0, 1)]
+        w1_raw = {(0, 0): load_w1(0, 0), (0, 1): load_w1_pieces(0, 1)}
         place_rows(v_plane[1][:], picked_rows, 1)
-        w1_raw = {(1, 0): load_halves(1, 0), (1, 1): [load_weight(w1, 1, KP, KP, "w1_raw11")[:]]}
-        ws_raw = [load_weight(wskip, a, 0, N, "ws_raw%d" % a)[:] for a in range(2)]
-        for a in range(2):
-            place_rows(w4_plane[:, a, :], w4_rows_dealt, a)
+        w1_raw[1, 0] = load_w1_pieces(1, 0)
+        w1_raw[1, 1] = load_w1(1, 1)
+        ws_raw = [load_weight(wskip, a, 0, N, "ws_raw%d" % a) for a in range(PASSES)]
+        for b in range(PASSES):
+            place_rows(w4_plane[:, b, :], w4_rows_dealt, b)
         nc.sync.dma_start(p1[:], pos1)
         nc.sync.dma_start(p2[:], pos2)
         nc.sync.dma_start(out=base_sb[:], in_=base.rearrange("(p t) -> p t", t=PACK))
 
-        slope = held([P, 2, PACK], F32, "slope")
+        slope = held([P, PASSES, PACK], F32, "slope")
         nc.vector.tensor_tensor(slope[:], fold_sb[:], gain_sb[:], ALU.mult)
 
         def round_and_deal(copy, rounded, raw, m0, slices):
@@ -128,138 +141,133 @@ def tile_list_broadloom_shade_pairs_kernel(
         def new_rounded():
             return passing([P, PACK * KP], BF16, "w_rounded")
 
-        v_words = [[held([P, BANK], U32, "v_words%d%d" % (a, c)) for c in range(2)] for a in range(2)]
+        def places(slices):
+            return slice(P * slices.start, P * slices.stop)
 
-        def gather_words(a, c):
-            window = tab[a][:].bitcast(U32)
-            nc.vector.tensor_copy(v_words[a][c][:], window.indirect(idx[:, 32 * c : 32 * (c + 1)]))
+        v_words = [[held([P, BANK], U32, "v_words%d%d" % (a, c)) for c in range(S // BANK)] for a in range(PASSES)]
 
         def v_operand(a, col0, width):
             c, off = divmod(col0, BANK)
             return v_words[a][c][:, off : off + width].bitcast(FP8X4), v_plane[a][:, col0 : col0 + width]
 
-        w1q = {(b, a): weight_tiles("w1q%d%d" % (b, a)) for b in range(2) for a in range(2)}
-        wsq = [weight_tiles("wsq%d" % a) for a in range(2)]
+        w1q = {(b, a): weight_tiles("w1q%d%d" % (b, a)) for b in range(PASSES) for a in range(PASSES)}
+        wsq = [weight_tiles("wsq%d" % a) for a in range(PASSES)]
 
-        gather_words(0, 0)
-        gather_words(0, 1)
-        gather_words(1, 0)
-        gather_words(1, 1)
-        for a in range(2):
+        for a in range(PASSES):
+            for c in range(S // BANK):
+                entries = idx[:, BANK // LIST * c : BANK // LIST * (c + 1)]
+                nc.vector.tensor_copy(v_words[a][c][:], tab[a][:].bitcast(U32).indirect(entries))
+
+        def round_w1(b, a):
             rounded = new_rounded()
-            for h, piece in enumerate(w1_first[a]):
-                if a == 0:
-                    round_and_deal(nc.vector.tensor_copy, rounded, piece, 0, slice(0, 4))
-                else:
-                    round_and_deal(nc.scalar.copy, rounded, piece, 64 * h, slice(0, 2))
-                    round_and_deal(nc.vector.tensor_copy, rounded, piece, 64 * h, slice(2, 4))
-            if a == 0:
-                quantise(rounded[:], w1q[0, a][0][:], w1q[0, a][1][:])
-            else:
-                for lo in (256, 0):
-                    quantise(rounded[:, 4 * lo : 4 * lo + 1024], w1q[0, a][0][:, lo : lo + 256], w1q[0, a][1][:, lo : lo + 256])
+            for i, piece in enumerate(w1_raw[b, a]):
+                round_and_deal(nc.vector.tensor_copy, rounded, piece, PIECE // PACK * i, ALL)
+            return rounded[:], w1q[b, a][0][:], w1q[b, a][1][:]
 
-        h_codes = {(b, c): held([P, BANK], U32, "h_codes%d%d" % (b, c)) for b in range(2) for c in range(2)}
-        h_plane = {(b, c): held([P, BANK], U8, "h_plane%d%d" % (b, c)) for b in range(2) for c in range(2)}
+        quantise(*round_w1(0, 0))
+        rounded = new_rounded()
+        for i, piece in enumerate(w1_raw[0, 1]):
+            round_and_deal(nc.scalar.copy, rounded, piece, PIECE // PACK * i, LOW)
+            round_and_deal(nc.vector.tensor_copy, rounded, piece, PIECE // PACK * i, HIGH)
+        for slices in (HIGH, LOW):
+            cols = places(slices)
+            values = rounded[:, PACK * cols.start : PACK * cols.stop]
+            quantise(values, w1q[0, 1][0][:, cols], w1q[0, 1][1][:, cols])
 
-        units = [(b, col0) for b in range(2) for col0 in range(0, S, UNIT)]
+        h_codes = {(b, c): held([P, BANK], U32, "h_codes%d%d" % (b, c)) for b in range(PASSES) for c in range(S // BANK)}
+        h_plane = {(b, c): held([P, BANK], U8, "h_plane%d%d" % (b, c)) for b in range(PASSES) for c in range(S // BANK)}
+
+        steps = [(b, col0) for b in range(PASSES) for col0 in range(0, S, STEP)]
+        last = len(steps) - 1
         banks, signs, factors, h_rounded = {}, {}, {}, {}
 
-        def new_quarter():
-            return ring.tile([P, UNIT * PACK], BF16, name="to_quantise", align_bytes=64, bufs=2)
+        def new_to_quantise():
+            return ring.tile([P, STEP * PACK], BF16, name="to_quantise", align_bytes=64, bufs=2)
 
         def multiply(u):
-            b, col0 = units[u]
-            banks[u] = [psum.tile([P, PACK, P], F32, name="bank") for h in range(2)]
-            for a in range(2):
+            b, col0 = steps[u]
+            banks[u] = [psum.tile([P, PACK, P], F32, name="bank") for i in range(STEP // P)]
+            for a in range(PASSES):
                 codes, plane = w1q[b, a]
-                for h in range(2):
-                    rhs, rhs_scale = v_operand(a, col0 + P * h, P)
+                for i, bank in enumerate(banks[u]):
+                    rhs, rhs_scale = v_operand(a, col0 + P * i, P)
                     for t in range(PACK):
                         nc.tensor.matmul_mx(
-                            out=banks[u][h][:, t, :],
+                            out=bank[:, t, :],
                             lhsT=codes[:, P * t : P * (t + 1)].bitcast(FP8X4),
                             lhsT_scale=plane[:, P * t : P * (t + 1)],
                             rhs=rhs,
                             rhs_scale=rhs_scale,
                             start=(a == 0 and t == 0),
-                            stop=(a == 1 and t == PACK - 1),
+                            stop=(a == PASSES - 1 and t == PACK - 1),
                         )
-            signs[u] = passing([P, PACK, UNIT], BF16, "sign")
+            signs[u] = passing([P, PACK, STEP], BF16, "sign")
 
-        def take_sign(u, h):
-            nc.scalar.activation(signs[u][:, :, P * h : P * (h + 1)], banks[u][h][:], ACT.Sign)
+        def take_sign(u, i):
+            nc.scalar.activation(signs[u][:, :, P * i : P * (i + 1)], banks[u][i][:], ACT.Sign)
 
         def make_factor(u):
-            b = units[u][0]
-            factors[u] = passing([P, PACK, UNIT], F32, "factor")
+            b = steps[u][0]
+            factors[u] = passing([P, PACK, STEP], F32, "factor")
             for t in range(PACK):
-                if u in (0, len(units) - 1):
-                    nc.vector.tensor_scalar(
-                        factors[u][:, t, :], signs[u][:, t, :], slope[:, b, t : t + 1], gain_sb[:, b, t : t + 1],
-                        ALU.mult, ALU.add,
-                    )
+                slope_t, gain_t = slope[:, b, t : t + 1], gain_sb[:, b, t : t + 1]
+                if u in (0, last):
+                    nc.vector.tensor_scalar(factors[u][:, t, :], signs[u][:, t, :], slope_t, gain_t, ALU.mult, ALU.add)
                 else:
-                    nc.scalar.activation(
-                        factors[u][:, t, :], signs[u][:, t, :], ACT.Identity,
-                        bias=gain_sb[:, b, t : t + 1], scale=slope[:, b, t : t + 1],
-                    )
-            h_rounded[u] = new_quarter()[:].rearrange("p (n t) -> p n t", t=PACK)
+                    nc.scalar.activation(factors[u][:, t, :], signs[u][:, t, :], ACT.Identity, bias=gain_t, scale=slope_t)
+            h_rounded[u] = new_to_quantise()[:].rearrange("p (n t) -> p n t", t=PACK)
 
-        def bend(u, h):
-            cols = slice(P * h, P * (h + 1))
+        def bend(u, i):
+            cols = slice(P * i, P * (i + 1))
             nc.vector.tensor_tensor(
-                h_rounded[u][:, cols, :].rearrange("p (c i) t -> p c t i", i=4),
-                banks[u][h][:].rearrange("p t (c i) -> p c t i", i=4),
-                factors[u][:, :, cols].rearrange("p t (c i) -> p c t i", i=4),
+                h_rounded[u][:, cols, :].rearrange("p (c e) t -> p c t e", e=RUN),
+                banks[u][i][:].rearrange("p t (c e) -> p c t e", e=RUN),
+                factors[u][:, :, cols].rearrange("p t (c e) -> p c t e", e=RUN),
                 ALU.mult,
             )
 
         def quantise_response(u):
-            b, col0 = units[u]
+            b, col0 = steps[u]
             c, off = divmod(col0, BANK)
             quantise(
                 h_rounded[u].rearrange("p n t -> p (n t)"),
-                h_codes[b, c][:, off : off + UNIT],
-                h_plane[b, c][:, off : off + UNIT],
+                h_codes[b, c][:, off : off + STEP],
+                h_plane[b, c][:, off : off + STEP],
             )
 
-
-        def round_w1(a):
-            rounded = new_rounded()
-            for h, piece in enumerate(w1_raw[1, a]):
-                round_and_deal(nc.vector.tensor_copy, rounded, piece, 64 * h, slice(0, PACK))
-            return rounded[:], w1q[1, a][0][:], w1q[1, a][1][:]
-
-        def round_wskip(copy, rounded, a, pair):
+        def round_wskip(copy, rounded, a, slices):
             dst = rounded[:].rearrange("p (t m j) -> p m j t", t=2, j=PACK)
             src = ws_raw[a].rearrange("p j (m t) -> p m j t", t=PACK)
-            copy(out=dst, in_=src[:, :, :, 2 * pair : 2 * pair + 2])
-            cols = slice(2 * P * pair, 2 * P * (pair + 1))
+            copy(out=dst, in_=src[:, :, :, slices])
+            cols = places(slices)
             return rounded[:], wsq[a][0][:, cols], wsq[a][1][:, cols]
 
         multiply(0)
         take_sign(0, 0)
-        for u in range(len(units)):
+        for u in range(len(steps)):
             take_sign(u, 1)
-            if u + 1 < len(units):
+            if u < last:
                 multiply(u + 1)
                 take_sign(u + 1, 0)
             make_factor(u)
-            weight = None
-            if u in (0, 1):
-                weight = round_w1(u)
-            if u in (3, 4):
-                weight = round_wskip(nc.vector.tensor_copy, passing([P, UNIT * PACK], BF16, "ws_rounded"), u - 3, 0)
+            weights = []
+            if u in W1_STEPS:
+                weights.append(round_w1(1, W1_STEPS.index(u)))
+            if u in WSKIP_STEPS:
+                rounded = passing([P, STEP * PACK], BF16, "ws_rounded")
+                weights.append(round_wskip(nc.vector.tensor_copy, rounded, WSKIP_STEPS.index(u), LOW))
             bend(u, 0)
             if u > 0:
                 quantise_response(u - 1)
             bend(u, 1)
-            if weight is not None:
+            for weight in weights:
                 quantise(*weight)
-        quantise_response(len(units) - 1)
-        late = [round_wskip(nc.scalar.copy, new_quarter(), 0, 1), round_wskip(nc.vector.tensor_copy, new_quarter(), 1, 1)]
-        for weight in late:
+        quantise_response(last)
+        weights = [
+            round_wskip(nc.scalar.copy, new_to_quantise(), 0, HIGH),
+            round_wskip(nc.vector.tensor_copy, new_to_quantise(), 1, HIGH),
+        ]
+        for weight in weights:
             quantise(*weight)
 
         y = held([P, 2, PACK, HALF], F32, "y")
@@ -269,76 +277,77 @@ def tile_list_broadloom_shade_pairs_kernel(
         out_words = out_1[0].rearrange("p m t -> p (m t)").bitcast(I32)
 
         def features(t):
-            g2 = held([P, S], F32, "g2_%d" % t)
-            for c in range(2):
+            g2_t = held([P, S], F32, "g2_%d" % t)
+            cols = slice(P * t, P * (t + 1))
+            for c in range(S // BANK):
                 bank = psum.tile([P, BANK], F32, name="bank")
-                for a in range(2):
-                    rhs, rhs_scale = v_operand(a, BANK * c, BANK)
+                skip, through = [], []
+                for a in range(PASSES):
+                    codes, plane = wsq[a]
+                    skip.append((codes[:, cols].bitcast(FP8X4), plane[:, cols]) + v_operand(a, BANK * c, BANK))
+                for b in range(PASSES):
+                    words = w4_codes[:, b, 2 * cols.start : 2 * cols.stop].bitcast(FP4X4)
+                    through.append((words, w4_plane[:, b, cols], h_codes[b, c][:].bitcast(FP8X4), h_plane[b, c][:]))
+                passes = skip + through if t < HIGH.start else through + skip
+                for i, (lhsT, lhsT_scale, rhs, rhs_scale) in enumerate(passes):
                     nc.tensor.matmul_mx(
                         out=bank[:],
-                        lhsT=wsq[a][0][:, P * t : P * (t + 1)].bitcast(FP8X4),
-                        lhsT_scale=wsq[a][1][:, P * t : P * (t + 1)],
+                        lhsT=lhsT,
+                        lhsT_scale=lhsT_scale,
                         rhs=rhs,
                         rhs_scale=rhs_scale,
-                        start=(a == 0),
-                        stop=False,
+                        start=(i == 0),
+                        stop=(i == len(passes) - 1),
                     )
-                for b in range(2):
-                    nc.tensor.matmul_mx(
-                        out=bank[:],
-                        lhsT=w4_codes[:, b, 2 * P * t : 2 * P * (t + 1)].bitcast(FP4X4),
-                        lhsT_scale=w4_plane[:, b, P * t : P * (t + 1)],
-                        rhs=h_codes[b, c][:].bitcast(FP8X4),
-                        rhs_scale=h_plane[b, c][:],
-                        start=False,
-                        stop=(b == 1),
-                    )
-                nc.scalar.copy(g2[:, BANK * c : BANK * (c + 1)], bank[:])
-            return g2
+                nc.scalar.copy(g2_t[:, BANK * c : BANK * (c + 1)], bank[:])
+            return g2_t
 
-        def pick(t, g2, m0, count):
+        def pick(t, m0, count):
             first = passing([P, count], F32, "first")
             second = passing([P, count], F32, "second")
             raised = passing([P, count], F32, "raised")
-            cols = slice(m0 // 16, (m0 + count) // 16)
-            nc.vector.tensor_copy(first[:], g2[:].indirect(p1[:, cols]))
-            nc.vector.tensor_copy(second[:], g2[:].indirect(p2[:, cols]))
+            cols = slice(m0 // LIST, (m0 + count) // LIST)
+            nc.vector.tensor_copy(first[:], g2[t][:].indirect(p1[:, cols]))
+            nc.vector.tensor_copy(second[:], g2[t][:].indirect(p2[:, cols]))
             nc.scalar.activation(raised[:], first[:], ACT.Identity, bias=base_sb[:, t : t + 1])
             halves = y[:, m0 // HALF : (m0 + count) // HALF, t, :]
             nc.vector.scalar_tensor_tensor(
                 halves,
-                second[:].rearrange("p (h m) -> p h m", m=HALF),
+                second[:].rearrange("p (i m) -> p i m", m=HALF),
                 base_sb[:, t : t + 1],
-                raised[:].rearrange("p (h m) -> p h m", m=HALF),
+                raised[:].rearrange("p (i m) -> p i m", m=HALF),
                 ALU.add,
                 ALU.min,
             )
-            nc.sync.dma_start(out=out_rows[:, t, m0 : m0 + count].rearrange("p (h m) -> p h m", m=HALF), in_=halves)
+            nc.sync.dma_start(out=out_rows[:, t, m0 : m0 + count].rearrange("p (i m) -> p i m", m=HALF), in_=halves)
 
-        def round_pairs(copy, rounded, h, m0, count):
+        def round_pairs(copy, i, cols):
             copy(
-                out=rounded[:, m0 : m0 + count, :].rearrange("p (c i) t -> p c t i", i=4),
-                in_=y[:, h, :, m0 : m0 + count].rearrange("p t (c i) -> p c t i", i=4),
+                out=y_rounded[i][:, cols, :].rearrange("p (c e) t -> p c t e", e=RUN),
+                in_=y[:, i, :, cols].rearrange("p t (c e) -> p c t e", e=RUN),
             )
 
-        def store_planes(h, rounded):
-            cols = slice(HALF * h, HALF * (h + 1))
-            quantise(rounded[:].rearrange("p m t -> p (m t)"), y_codes[:, cols], y_plane[:, cols])
+        def store_words(i):
+            cols = slice(HALF * i, HALF * (i + 1))
+            quantise(y_rounded[i][:].rearrange("p m t -> p (m t)"), y_codes[:, cols], y_plane[:, cols])
             nc.sync.dma_start(out=out_words[:, cols], in_=y_codes[:, cols].bitcast(I32))
 
         g2 = [features(t) for t in range(PACK)]
-        for t in range(PACK - 1):
-            pick(t, g2[t], 0, PAIRS)
-        y_rounded = [held([P, HALF, PACK], BF16, "y_rounded%d" % h) for h in range(2)]
-        pick(PACK - 1, g2[PACK - 1], 0, HALF)
-        round_pairs(nc.scalar.copy, y_rounded[0], 0, 0, HALF)
-        pick(PACK - 1, g2[PACK - 1], HALF, HALF)
-        store_planes(0, y_rounded[0])
-        round_pairs(nc.vector.tensor_copy, y_rounded[1], 1, 0, HALF)
-        store_planes(1, y_rounded[1])
-        for q in range(4):
-            queue = nc.scalar if q % 2 == 0 else nc.sync
+        y_rounded = [held([P, HALF, PACK], BF16, "y_rounded%d" % i) for i in range(2)]
+        pick(0, 0, PAIRS)
+        pick(1, 0, PAIRS)
+        pick(2, 0, HALF)
+        pick(3, 0, HALF)
+        round_pairs(nc.scalar.copy, 0, slice(0, HALF))
+        pick(2, HALF, HALF)
+        store_words(0)
+        pick(3, HALF, HALF)
+        round_pairs(nc.vector.tensor_copy, 1, slice(0, VECTOR_SHARE))
+        round_pairs(nc.scalar.copy, 1, slice(VECTOR_SHARE, HALF))
+        store_words(1)
+        for quad in range(QUADS):
+            queue = nc.scalar if quad % 2 == 0 else nc.sync
             queue.dma_start(
-                out=out_2[0, 4 * q : 4 * q + 4, :].bitcast(I32),
-                in_=y_plane[32 * q : 32 * q + 4, :].bitcast(I32),
+                out=out_2[0, 4 * quad : 4 * quad + 4, :].bitcast(I32),
+                in_=y_plane[32 * quad : 32 * quad + 4, :].bitcast(I32),
             )

from contextlib import ExitStack

import concourse.mybir as mybir

T, S, PAIRS, K, H, N = 4096, 1024, 512, 1024, 1024, 512
FLOPS = 2 * S * (K * H + H * N + K * N)

F32 = mybir.dt.float32
BF16 = mybir.dt.bfloat16
I32 = mybir.dt.int32
U32 = mybir.dt.uint32
U16 = mybir.dt.uint16
U8 = mybir.dt.uint8
FP8X4 = mybir.dt.float8_e4m3fn_x4
FP4X4 = mybir.dt.float4_e2m1fn_x4
ALU = mybir.AluOpType
ACT = mybir.ActivationFunctionType

P = 128
PACK = 4
KP = P * PACK
PASSES = 2
BANK = 512
LIST = 16
QUADS = 4
STEP = 2 * P
HALF = PAIRS // 2
PIECE = KP // 2
RUN = 4
LOW, HIGH, ALL = slice(0, 2), slice(2, PACK), slice(0, PACK)
VECTOR_SHARE = 168
W1_STEPS = (0, 1)
WSKIP_STEPS = (3, 4)


def tile_list_broadloom_shade_pairs_kernel(
    tc, tab_words, tab_scales, offs, w1, fold, gain, w4_words, w4_scales, wskip, base, pos1, pos2,
    out_0, out_1, out_2,
):
    nc = tc.nc
    with ExitStack() as ctx:
        keep = ctx.enter_context(tc.tile_pool(name="keep", bufs=1))
        ring = ctx.enter_context(tc.tile_pool(name="ring", bufs=3))
        psum = ctx.enter_context(tc.psum_pool(name="psum", bufs=8))

        def held(shape, dtype, name):
            return keep.tile(shape, dtype, name=name, align_bytes=64)

        def passing(shape, dtype, name):
            return ring.tile(shape, dtype, name=name, align_bytes=64)

        idx = keep.tile([P, S // LIST], U16, name="idx")
        p1 = keep.tile([P, PAIRS // LIST], U16, name="p1")
        p2 = keep.tile([P, PAIRS // LIST], U16, name="p2")

        tab_rows = held([P, T], U8, "tab_rows")
        picked_rows = held([P, S], U8, "picked_rows")
        v_plane = [held([P, S], U8, "v_plane%d" % a) for a in range(PASSES)]
        w4_rows = held([P, N], U8, "w4_rows")
        w4_rows_dealt = held([P, N], U8, "w4_rows_dealt")
        w4_plane = held([P, PASSES, N], U8, "w4_plane")
        w4_raw = held([P, PASSES, 2 * N], U8, "w4_raw")
        w4_codes = held([P, PASSES, 2 * N], U8, "w4_codes")
        fold_sb = held([P, PASSES, PACK], F32, "fold_sb")
        gain_sb = held([P, PASSES, PACK], F32, "gain_sb")
        base_sb = held([P, PACK], F32, "base_sb")
        tab = [held([P, T], I32, "tab%d" % a) for a in range(PASSES)]
        for partly_loaded in (tab_rows, w4_rows, v_plane[0], v_plane[1], w4_plane):
            nc.vector.memset(partly_loaded[:].bitcast(I32), 0)

        def load_rows(rows, scales):
            nc.sync.dma_start(out=rows[0:P:4, :].bitcast(I32), in_=scales.rearrange("a q c -> (a q) c").bitcast(I32))

        def place_rows(plane, rows, a):
            for r in range(4):
                nc.sync.dma_start(
                    out=plane[r:P:32, :].bitcast(I32),
                    in_=rows[64 * a + 4 * r : 64 * (a + 1) : 16, :].bitcast(I32),
                )

        def load_tab(a):
            nc.sync.dma_start(out=tab[a][:], in_=tab_words[a].rearrange("p t i -> p (t i)").bitcast(I32))

        def load_weight(w, a, c0, width, name):
            raw = held([P, PACK, width], F32, name)
            rows = w[KP * a : KP * (a + 1), c0 : c0 + width]
            nc.sync.dma_start(out=raw[:], in_=rows.rearrange("(p j) c -> p j c", j=PACK))
            return raw[:]

        def load_w1(b, a):
            return [load_weight(w1, a, KP * b, KP, "w1_raw%d%d" % (b, a))]

        def load_w1_pieces(b, a):
            return [load_weight(w1, a, KP * b + PIECE * i, PIECE, "w1_raw%d%d%d" % (b, a, i)) for i in range(2)]

        nc.sync.dma_start(idx[:], offs)
        nc.sync.dma_start(out=w4_raw[:].bitcast(I32), in_=w4_words.bitcast(I32).rearrange("a p c -> p a c"))
        nc.sync.dma_start(out=fold_sb[:], in_=fold.rearrange("(b p t) -> p b t", b=PASSES, t=PACK))
        nc.sync.dma_start(out=gain_sb[:], in_=gain.rearrange("(b p t) -> p b t", b=PASSES, t=PACK))
        load_rows(tab_rows, tab_scales)
        load_rows(w4_rows, w4_scales)
        nc.vector.tensor_copy(picked_rows[:], tab_rows[:].indirect(idx[:]))
        for b in range(PASSES):
            nc.vector.tensor_copy(
                out=w4_codes[:, b, :].rearrange("p (t m e) -> p t m e", t=PACK, e=2),
                in_=w4_raw[:, b, :].rearrange("p (m t e) -> p t m e", t=PACK, e=2),
            )
        nc.vector.tensor_copy(
            out=w4_rows_dealt[:].rearrange("p (t m) -> p t m", t=PACK),
            in_=w4_rows[:].rearrange("p (m t) -> p t m", t=PACK),
        )
        load_tab(0)
        load_tab(1)
        place_rows(v_plane[0][:], picked_rows, 0)
        w1_raw = {(0, 0): load_w1(0, 0), (0, 1): load_w1_pieces(0, 1)}
        place_rows(v_plane[1][:], picked_rows, 1)
        w1_raw[1, 0] = load_w1_pieces(1, 0)
        w1_raw[1, 1] = load_w1(1, 1)
        ws_raw = [load_weight(wskip, a, 0, N, "ws_raw%d" % a) for a in range(PASSES)]
        for b in range(PASSES):
            place_rows(w4_plane[:, b, :], w4_rows_dealt, b)
        nc.sync.dma_start(p1[:], pos1)
        nc.sync.dma_start(p2[:], pos2)
        nc.sync.dma_start(out=base_sb[:], in_=base.rearrange("(p t) -> p t", t=PACK))

        slope = held([P, PASSES, PACK], F32, "slope")
        nc.vector.tensor_tensor(slope[:], fold_sb[:], gain_sb[:], ALU.mult)

        def round_and_deal(copy, rounded, raw, m0, slices):
            count = raw.shape[2] // PACK
            dst = rounded[:].rearrange("p (t m j) -> p m j t", t=PACK, j=PACK)
            src = raw.rearrange("p j (m t) -> p m j t", t=PACK)
            copy(out=dst[:, m0 : m0 + count, :, slices], in_=src[:, :, :, slices])

        def quantise(rounded, codes, plane):
            nc.vector.quantize_mx(out=codes.bitcast(FP8X4), scales=plane, in_=rounded)

        def weight_tiles(name):
            return held([P, KP], U32, name + "_codes"), held([P, KP], U8, name + "_plane")

        def new_rounded():
            return passing([P, PACK * KP], BF16, "w_rounded")

        def places(slices):
            return slice(P * slices.start, P * slices.stop)

        v_words = [[held([P, BANK], U32, "v_words%d%d" % (a, c)) for c in range(S // BANK)] for a in range(PASSES)]

        def v_operand(a, col0, width):
            c, off = divmod(col0, BANK)
            return v_words[a][c][:, off : off + width].bitcast(FP8X4), v_plane[a][:, col0 : col0 + width]

        w1q = {(b, a): weight_tiles("w1q%d%d" % (b, a)) for b in range(PASSES) for a in range(PASSES)}
        wsq = [weight_tiles("wsq%d" % a) for a in range(PASSES)]

        for a in range(PASSES):
            for c in range(S // BANK):
                entries = idx[:, BANK // LIST * c : BANK // LIST * (c + 1)]
                nc.vector.tensor_copy(v_words[a][c][:], tab[a][:].bitcast(U32).indirect(entries))

        def round_w1(b, a):
            rounded = new_rounded()
            for i, piece in enumerate(w1_raw[b, a]):
                round_and_deal(nc.vector.tensor_copy, rounded, piece, PIECE // PACK * i, ALL)
            return rounded[:], w1q[b, a][0][:], w1q[b, a][1][:]

        quantise(*round_w1(0, 0))
        rounded = new_rounded()
        for i, piece in enumerate(w1_raw[0, 1]):
            round_and_deal(nc.scalar.copy, rounded, piece, PIECE // PACK * i, LOW)
            round_and_deal(nc.vector.tensor_copy, rounded, piece, PIECE // PACK * i, HIGH)
        for slices in (HIGH, LOW):
            cols = places(slices)
            values = rounded[:, PACK * cols.start : PACK * cols.stop]
            quantise(values, w1q[0, 1][0][:, cols], w1q[0, 1][1][:, cols])

        h_codes = {(b, c): held([P, BANK], U32, "h_codes%d%d" % (b, c)) for b in range(PASSES) for c in range(S // BANK)}
        h_plane = {(b, c): held([P, BANK], U8, "h_plane%d%d" % (b, c)) for b in range(PASSES) for c in range(S // BANK)}

        steps = [(b, col0) for b in range(PASSES) for col0 in range(0, S, STEP)]
        last = len(steps) - 1
        banks, signs, factors, h_rounded = {}, {}, {}, {}

        def new_to_quantise():
            return ring.tile([P, STEP * PACK], BF16, name="to_quantise", align_bytes=64, bufs=2)

        def multiply(u):
            b, col0 = steps[u]
            banks[u] = [psum.tile([P, PACK, P], F32, name="bank") for i in range(STEP // P)]
            for a in range(PASSES):
                codes, plane = w1q[b, a]
                for i, bank in enumerate(banks[u]):
                    rhs, rhs_scale = v_operand(a, col0 + P * i, P)
                    for t in range(PACK):
                        nc.tensor.matmul_mx(
                            out=bank[:, t, :],
                            lhsT=codes[:, P * t : P * (t + 1)].bitcast(FP8X4),
                            lhsT_scale=plane[:, P * t : P * (t + 1)],
                            rhs=rhs,
                            rhs_scale=rhs_scale,
                            start=(a == 0 and t == 0),
                            stop=(a == PASSES - 1 and t == PACK - 1),
                        )
            signs[u] = passing([P, PACK, STEP], BF16, "sign")

        def take_sign(u, i):
            nc.scalar.activation(signs[u][:, :, P * i : P * (i + 1)], banks[u][i][:], ACT.Sign)

        def make_factor(u):
            b = steps[u][0]
            factors[u] = passing([P, PACK, STEP], F32, "factor")
            for t in range(PACK):
                slope_t, gain_t = slope[:, b, t : t + 1], gain_sb[:, b, t : t + 1]
                if u in (0, last):
                    nc.vector.tensor_scalar(factors[u][:, t, :], signs[u][:, t, :], slope_t, gain_t, ALU.mult, ALU.add)
                else:
                    nc.scalar.activation(factors[u][:, t, :], signs[u][:, t, :], ACT.Identity, bias=gain_t, scale=slope_t)
            h_rounded[u] = new_to_quantise()[:].rearrange("p (n t) -> p n t", t=PACK)

        def bend(u, i):
            cols = slice(P * i, P * (i + 1))
            nc.vector.tensor_tensor(
                h_rounded[u][:, cols, :].rearrange("p (c e) t -> p c t e", e=RUN),
                banks[u][i][:].rearrange("p t (c e) -> p c t e", e=RUN),
                factors[u][:, :, cols].rearrange("p t (c e) -> p c t e", e=RUN),
                ALU.mult,
            )

        def quantise_response(u):
            b, col0 = steps[u]
            c, off = divmod(col0, BANK)
            quantise(
                h_rounded[u].rearrange("p n t -> p (n t)"),
                h_codes[b, c][:, off : off + STEP],
                h_plane[b, c][:, off : off + STEP],
            )

        def round_wskip(copy, rounded, a, slices):
            dst = rounded[:].rearrange("p (t m j) -> p m j t", t=2, j=PACK)
            src = ws_raw[a].rearrange("p j (m t) -> p m j t", t=PACK)
            copy(out=dst, in_=src[:, :, :, slices])
            cols = places(slices)
            return rounded[:], wsq[a][0][:, cols], wsq[a][1][:, cols]

        multiply(0)
        take_sign(0, 0)
        for u in range(len(steps)):
            take_sign(u, 1)
            if u < last:
                multiply(u + 1)
                take_sign(u + 1, 0)
            make_factor(u)
            weights = []
            if u in W1_STEPS:
                weights.append(round_w1(1, W1_STEPS.index(u)))
            if u in WSKIP_STEPS:
                rounded = passing([P, STEP * PACK], BF16, "ws_rounded")
                weights.append(round_wskip(nc.vector.tensor_copy, rounded, WSKIP_STEPS.index(u), LOW))
            bend(u, 0)
            if u > 0:
                quantise_response(u - 1)
            bend(u, 1)
            for weight in weights:
                quantise(*weight)
        quantise_response(last)
        weights = [
            round_wskip(nc.scalar.copy, new_to_quantise(), 0, HIGH),
            round_wskip(nc.vector.tensor_copy, new_to_quantise(), 1, HIGH),
        ]
        for weight in weights:
            quantise(*weight)

        y = held([P, 2, PACK, HALF], F32, "y")
        y_codes = held([P, PAIRS], U32, "y_codes")
        y_plane = held([P, PAIRS], U8, "y_plane")
        out_rows = out_0.rearrange("(p t) m -> p t m", t=PACK)
        out_words = out_1[0].rearrange("p m t -> p (m t)").bitcast(I32)

        def features(t):
            g2_t = held([P, S], F32, "g2_%d" % t)
            cols = slice(P * t, P * (t + 1))
            for c in range(S // BANK):
                bank = psum.tile([P, BANK], F32, name="bank")
                skip, through = [], []
                for a in range(PASSES):
                    codes, plane = wsq[a]
                    skip.append((codes[:, cols].bitcast(FP8X4), plane[:, cols]) + v_operand(a, BANK * c, BANK))
                for b in range(PASSES):
                    words = w4_codes[:, b, 2 * cols.start : 2 * cols.stop].bitcast(FP4X4)
                    through.append((words, w4_plane[:, b, cols], h_codes[b, c][:].bitcast(FP8X4), h_plane[b, c][:]))
                passes = skip + through if t < HIGH.start else through + skip
                for i, (lhsT, lhsT_scale, rhs, rhs_scale) in enumerate(passes):
                    nc.tensor.matmul_mx(
                        out=bank[:],
                        lhsT=lhsT,
                        lhsT_scale=lhsT_scale,
                        rhs=rhs,
                        rhs_scale=rhs_scale,
                        start=(i == 0),
                        stop=(i == len(passes) - 1),
                    )
                nc.scalar.copy(g2_t[:, BANK * c : BANK * (c + 1)], bank[:])
            return g2_t

        def pick(t, m0, count):
            first = passing([P, count], F32, "first")
            second = passing([P, count], F32, "second")
            raised = passing([P, count], F32, "raised")
            cols = slice(m0 // LIST, (m0 + count) // LIST)
            nc.vector.tensor_copy(first[:], g2[t][:].indirect(p1[:, cols]))
            nc.vector.tensor_copy(second[:], g2[t][:].indirect(p2[:, cols]))
            nc.scalar.activation(raised[:], first[:], ACT.Identity, bias=base_sb[:, t : t + 1])
            halves = y[:, m0 // HALF : (m0 + count) // HALF, t, :]
            nc.vector.scalar_tensor_tensor(
                halves,
                second[:].rearrange("p (i m) -> p i m", m=HALF),
                base_sb[:, t : t + 1],
                raised[:].rearrange("p (i m) -> p i m", m=HALF),
                ALU.add,
                ALU.min,
            )
            nc.sync.dma_start(out=out_rows[:, t, m0 : m0 + count].rearrange("p (i m) -> p i m", m=HALF), in_=halves)

        def round_pairs(copy, i, cols):
            copy(
                out=y_rounded[i][:, cols, :].rearrange("p (c e) t -> p c t e", e=RUN),
                in_=y[:, i, :, cols].rearrange("p t (c e) -> p c t e", e=RUN),
            )

        def store_words(i):
            cols = slice(HALF * i, HALF * (i + 1))
            quantise(y_rounded[i][:].rearrange("p m t -> p (m t)"), y_codes[:, cols], y_plane[:, cols])
            nc.sync.dma_start(out=out_words[:, cols], in_=y_codes[:, cols].bitcast(I32))

        g2 = [features(t) for t in range(PACK)]
        y_rounded = [held([P, HALF, PACK], BF16, "y_rounded%d" % i) for i in range(2)]
        pick(0, 0, PAIRS)
        pick(1, 0, PAIRS)
        pick(2, 0, HALF)
        pick(3, 0, HALF)
        round_pairs(nc.scalar.copy, 0, slice(0, HALF))
        pick(2, HALF, HALF)
        store_words(0)
        pick(3, HALF, HALF)
        round_pairs(nc.vector.tensor_copy, 1, slice(0, VECTOR_SHARE))
        round_pairs(nc.scalar.copy, 1, slice(VECTOR_SHARE, HALF))
        store_words(1)
        for quad in range(QUADS):
            queue = nc.scalar if quad % 2 == 0 else nc.sync
            queue.dma_start(
                out=out_2[0, 4 * quad : 4 * quad + 4, :].bitcast(I32),
                in_=y_plane[32 * quad : 32 * quad + 4, :].bitcast(I32),
            )
